import numpy as np
import ml_dtypes


def mxq(x, axis, fmt="e4m3"):
    dtype, down = {"e4m3": (ml_dtypes.float8_e4m3fn, 7), "e5m2": (ml_dtypes.float8_e5m2, 14)}[fmt]
    v = np.moveaxis(np.asarray(x, np.float32).astype(ml_dtypes.bfloat16).astype(np.float64), axis, -1)
    blocks = v.reshape(v.shape[:-1] + (-1, 32))
    amax = np.abs(blocks).max(-1, keepdims=True)
    byte = np.maximum(np.where(amax > 0, np.frexp(amax)[1] - 1 + 127, 0) - down, 1)
    scale = np.exp2(byte - 127.0)
    codes = (blocks / scale).astype(np.float32).astype(dtype).astype(np.float64)
    return np.moveaxis((codes * scale).reshape(v.shape), -1, axis)


WIDE = False


def mx_kscale(k):
    if not WIDE:
        return np.ones(k)
    levels = np.array([10, -10, 5, -5, 0])
    if k % 512:
        return np.exp2(np.random.permutation(np.resize(levels, k // 32))).repeat(32)
    a = np.empty((k // 512, 16))
    for p in range(k // 512):
        a[p, :8] = np.random.permutation(np.resize(levels, 8))
        for g in range(8):
            far = levels[np.abs(levels - a[p, g]) >= 10]
            a[p, g + 8] = far[np.random.randint(len(far))]
    return np.exp2(a.ravel()).repeat(32)


def f64(x):
    return np.asarray(x).astype(np.float64)


def striped(idx):
    return np.tile(idx.reshape(-1, 16).T, (8, 1)).astype(np.uint16)


def unstriped(offs):
    return offs[:16].T.reshape(-1).astype(np.int64)


def striped8(idx):
    return np.concatenate([v.reshape(-1, 16).T for v in idx]).astype(np.uint16)


def unstriped8(offs):
    return np.stack([offs[16 * g:16 * g + 16].T.reshape(-1) for g in range(8)]).astype(np.int64)


E2M1 = np.array([0.0, 0.5, 1.0, 1.5, 2.0, 3.0, 4.0, 6.0, -0.0, -0.5, -1.0, -1.5, -2.0, -3.0, -4.0, -6.0])


def pack_weight(w, fmt):
    k, n = w.shape
    w = f64(np.asarray(w, np.float32).astype(ml_dtypes.bfloat16)).reshape(k // 32, 32, n)
    amax = np.abs(w).max(1)
    if fmt == "e4m3":
        byte = np.frexp(amax)[1] - 1 + 127 - 7
    else:
        mant, ex = np.frexp(amax / 6.0)
        byte = np.where(mant > 0.5, ex, ex - 1) + 127
    byte = np.clip(np.where(amax > 0, byte, 1), 1, 254)
    scaled = (w * np.exp2(127.0 - byte)[:, None, :]).reshape(k, n).astype(np.float32)
    by_word = np.ascontiguousarray(scaled.reshape(k // 512, 128, 4, n).transpose(0, 1, 3, 2))
    if fmt == "e4m3":
        words = by_word.astype(ml_dtypes.float8_e4m3fn).view(np.uint8)
    else:
        c = by_word.astype(ml_dtypes.float4_e2m1fn).view(np.uint8) & 0xF
        words = (c[..., 0::2] | (c[..., 1::2] << 4)).reshape(k // 512, 128, 2 * n)
    return np.ascontiguousarray(words), np.ascontiguousarray(byte.astype(np.uint8).reshape(k // 512, 16, n))


def unpack_weight(words, scales, fmt):
    g, _, n = scales.shape
    words = np.ascontiguousarray(words).reshape(g, 128, n, -1)
    if fmt == "e4m3":
        vals = words.view(ml_dtypes.float8_e4m3fn).astype(np.float64)
    else:
        nib = np.empty((g, 128, n, 4), np.uint8)
        nib[..., 0::2] = words & 0xF
        nib[..., 1::2] = words >> 4
        vals = E2M1[nib]
    vals = vals * np.repeat(np.exp2(scales.astype(np.float64) - 127.0), 8, axis=1)[..., None]
    return vals.transpose(0, 1, 3, 2).reshape(g * 512, n)


def pack_table(v):
    words, scales = pack_weight(v, "e4m3")
    return np.concatenate([words.reshape(words.shape[0], -1), scales.reshape(scales.shape[0], -1)], axis=1)


def unpack_table(tab):
    g, t = tab.shape[0], tab.shape[1] // 528
    return unpack_weight(tab[:, :512 * t].reshape(g, 128, t, 4), tab[:, 512 * t:].reshape(g, 16, t), "e4m3")


def gelu(v):
    return 0.5 * v * (1.0 + np.tanh(np.sqrt(2.0 / np.pi) * (v + 0.044715 * v**3)))


K, M, T, S = 1536, 128, 4096, 2048


def setup_inputs():
    n = np.random.standard_normal
    s = mx_kscale(K)[:, None]
    w = n((K, M)) / np.sqrt(K) / s
    p_w4 = pack_weight(w[512:], "e2m1")
    return {
        "tab": pack_table(n((K, T)) * s),
        "w8": (w[:512]).astype(np.float32),
        "w4_words": p_w4[0],
        "w4_scales": p_w4[1],
        "b": (0.3 * n(128)).astype(np.float32),
        "wgo": np.repeat(np.random.uniform(0.5, 2.0, (8, S)), 16, axis=0).astype(np.float32),
        "offs": striped(np.random.permutation(T)[:S]),
        "offs2": striped8(np.stack([np.random.permutation(T)[:S] for _ in range(8)])),
    }


def reference(tab, w8, w4_words, w4_scales, b, wgo, offs, offs2):
    tab_ = unpack_table(tab)[:, unstriped(offs)]
    w8_ = mxq(f64(w8), 0, "e4m3")
    w4_ = unpack_weight(w4_words, w4_scales, "e2m1")
    y = w8_.T @ tab_[:512] + w4_.T @ tab_[512:]
    place = unstriped8(offs2)[np.arange(M) % 128 // 16]
    out = np.zeros((M, T))
    out[np.arange(M)[:, None], place] = f64(wgo)[np.arange(M) % 128] * (gelu(y + f64(b)[:, None]))
    return out

@@ -1,0 +1,156 @@
+from contextlib import ExitStack
+
+import concourse.mybir as mybir
+
+K, M, T, S = 1536, 128, 4096, 2048
+FLOPS = 2 * K * M * S
+
+F32 = mybir.dt.float32
+BF16 = mybir.dt.bfloat16
+I32 = mybir.dt.int32
+U32 = mybir.dt.uint32
+U16 = mybir.dt.uint16
+U8 = mybir.dt.uint8
+FP8X4 = mybir.dt.float8_e4m3fn_x4
+FP4X4 = mybir.dt.float4_e2m1fn_x4
+
+P = 128
+PACK = 4
+PASSES = 3
+BANK = 512
+HALF = S // 2
+QUADS = 4
+
+
+def tile_list_tabhs_o_gelu_kernel(
+    tc, tab, w8, w4_words, w4_scales, b, wgo, offs, offs2, out
+):
+    nc = tc.nc
+    with ExitStack() as ctx:
+        keep = ctx.enter_context(tc.tile_pool(name="keep", bufs=1))
+        psum = ctx.enter_context(tc.psum_pool(name="psum", bufs=1))
+
+        pick = keep.tile([P, S // 16], U16, name="pick")
+        place = keep.tile([P, S // 16], U16, name="place")
+        scale_win = keep.tile([P, T], U8, name="scale_win", align_bytes=64)
+        words = [keep.tile([P, T], U32, name="words%d" % a, align_bytes=64) for a in range(PASSES)]
+        page = keep.tile([P, T], F32, name="page", align_bytes=64)
+        plane01 = keep.tile([P, S], U8, name="plane01", align_bytes=64)
+        plane2 = keep.tile([P, S], U8, name="plane2", align_bytes=64)
+        w4_codes = keep.tile([P, 2, 2 * M], U8, name="w4_codes", align_bytes=64)
+        w4_plane = keep.tile([P, 2, M], U8, name="w4_plane", align_bytes=64)
+        bias = keep.tile([P, 1], F32, name="bias")
+        w8_raw = keep.tile([P, PACK, M], F32, name="w8_raw", tag="w8_then_wgo0", align_bytes=64)
+        w8_bf = keep.tile([P, M, PACK], BF16, name="w8_bf", tag="w8_then_wgo1", align_bytes=64)
+        w8_codes = keep.tile([P, M], U32, name="w8_codes", align_bytes=64)
+        w8_plane = keep.tile([P, M], U8, name="w8_plane", align_bytes=64)
+
+        win32 = scale_win[:].bitcast(I32)
+        rows_of_pass = [slice(0, 32, 2), slice(1, 32, 2), slice(112, 128, 1)]
+
+        def load_words(a):
+            src = tab[a, 0 : 512 * T].rearrange("(p n) -> p n", p=P).bitcast(I32)
+            nc.sync.dma_start(out=words[a][:].bitcast(I32), in_=src)
+
+        nc.vector.memset(win32[32:64, :], 0)
+        nc.vector.memset(win32[64:112, :], 0)
+        nc.gpsimd.memset(w4_plane[:].rearrange("p a n -> p (a n)").bitcast(I32), 0)
+        nc.gpsimd.memset(plane01[:].bitcast(I32), 0)
+        nc.gpsimd.memset(plane2[:].bitcast(I32), 0)
+
+        nc.sync.dma_start(pick[:], offs)
+        for a in (2, 0, 1):
+            src = tab[a, 512 * T : 528 * T].rearrange("(q t) -> q t", q=16).bitcast(I32)
+            nc.sync.dma_start(out=win32[rows_of_pass[a], :], in_=src)
+        load_words(0)
+        nc.sync.dma_start(out=w8_raw[:], in_=w8.rearrange("(p j) n -> p j n", j=PACK))
+        load_words(1)
+        nc.sync.dma_start(place[:], offs2)
+        load_words(2)
+
+        w4_plane32 = w4_plane[:].bitcast(I32)
+        for q in range(QUADS):
+            src = w4_scales[:, 4 * q : 4 * q + 4, :].rearrange("a r n -> r a n").bitcast(I32)
+            nc.gpsimd.dma_start(out=w4_plane32[32 * q : 32 * q + 4, :, :], in_=src)
+        nc.gpsimd.dma_start(
+            out=w4_codes[:].bitcast(I32), in_=w4_words.rearrange("a p n -> p a n").bitcast(I32)
+        )
+        nc.gpsimd.dma_start(out=bias[:], in_=b.rearrange("(p o) -> p o", o=1))
+        nc.gpsimd.memset(page[:], 0.0)
+
+        got_scales = keep.tile([P, S], U8, name="got_scales", align_bytes=64)
+        nc.vector.tensor_copy(got_scales[:], scale_win[:].indirect(pick[:]))
+        got32 = got_scales[:].bitcast(I32)
+        planes = [(plane01, 4), (plane01, 0), (plane2, 0)]
+        for a in range(PASSES):
+            plane, first = planes[a]
+            rows = rows_of_pass[a]
+            for q in range(QUADS):
+                lo = rows.start + 4 * q * rows.step
+                nc.sync.dma_start(
+                    out=plane[:].bitcast(I32)[32 * q + first : 32 * q + first + 4, :],
+                    in_=got32[lo : lo + 3 * rows.step + 1 : rows.step, :],
+                )
+
+        nc.scalar.copy(out=w8_bf[:], in_=w8_raw[:].rearrange("p j n -> p n j"))
+
+        got = [keep.tile([P, S], U32, name="got%d" % a, align_bytes=64) for a in range(2)]
+        got_last = [keep.tile([P, HALF], U32, name="got_last%d" % h, align_bytes=64) for h in range(2)]
+        nc.vector.tensor_copy(got[0][:], words[0][:].indirect(pick[:]))
+        nc.vector.quantize_mx(
+            out=w8_codes[:].bitcast(FP8X4),
+            scales=w8_plane[:],
+            in_=w8_bf[:].rearrange("p n j -> p (n j)"),
+        )
+        nc.vector.tensor_copy(got[1][:], words[1][:].indirect(pick[:]))
+        for h in range(2):
+            cols16 = slice(h * HALF // 16, (h + 1) * HALF // 16)
+            nc.vector.tensor_copy(got_last[h][:], words[2][:].indirect(pick[:, cols16]))
+
+        for h in range(2):
+            gain = keep.tile([P, HALF], F32, name="gain%d" % h, tag="w8_then_wgo%d" % h, align_bytes=64)
+            nc.sync.dma_start(out=gain[:], in_=wgo[:, h * HALF : (h + 1) * HALF])
+            act = keep.tile([P, HALF], F32, name="act%d" % h, align_bytes=64)
+            for s in range(HALF // BANK):
+                local = slice(s * BANK, (s + 1) * BANK)
+                cols = slice(h * HALF + s * BANK, h * HALF + (s + 1) * BANK)
+                acc = psum.tile([P, BANK], F32, name="acc%d_%d" % (h, s))
+                nc.tensor.matmul_mx(
+                    out=acc[:],
+                    lhsT=w8_codes[:].bitcast(FP8X4),
+                    lhsT_scale=w8_plane[:],
+                    rhs=got[0][:, cols].bitcast(FP8X4),
+                    rhs_scale=plane01[4:P, cols],
+                    start=True,
+                    stop=False,
+                )
+                nc.tensor.matmul_mx(
+                    out=acc[:],
+                    lhsT=w4_codes[:, 0, :].bitcast(FP4X4),
+                    lhsT_scale=w4_plane[:, 0, :],
+                    rhs=got[1][:, cols].bitcast(FP8X4),
+                    rhs_scale=plane01[:, cols],
+                    start=False,
+                    stop=False,
+                )
+                nc.tensor.matmul_mx(
+                    out=acc[:],
+                    lhsT=w4_codes[:, 1, :].bitcast(FP4X4),
+                    lhsT_scale=w4_plane[:, 1, :],
+                    rhs=got_last[h][:, local].bitcast(FP8X4),
+                    rhs_scale=plane2[:, cols],
+                    start=False,
+                    stop=True,
+                )
+                nc.scalar.activation(
+                    out=act[:, local],
+                    in_=acc[:],
+                    func=mybir.ActivationFunctionType.Gelu_apprx_tanh,
+                    bias=bias[:],
+                )
+            cols16 = slice(h * HALF // 16, (h + 1) * HALF // 16)
+            nc.vector.tensor_tensor(
+                page[:].indirect(place[:, cols16]), act[:], gain[:], mybir.AluOpType.mult
+            )
+
+        nc.sync.dma_start(out=out, in_=page[:])

@@ -32,8 +32,8 @@ def tile_list_tabhs_o_gelu_kernel(
 
         pick = keep.tile([P, S // 16], U16, name="pick")
         place = keep.tile([P, S // 16], U16, name="place")
-        scale_win = keep.tile([P, T], U8, name="scale_win", align_bytes=64)
-        words = [keep.tile([P, T], U32, name="words%d" % a, align_bytes=64) for a in range(PASSES)]
+        scale_win = keep.tile([P, T], U8, name="scale_win", tag="scales_then_words", align_bytes=64)
+        words = [keep.tile([P, T], U32, name="words%d" % a, align_bytes=64) for a in range(2)]
         page = keep.tile([P, T], F32, name="page", align_bytes=64)
         plane01 = keep.tile([P, S], U8, name="plane01", align_bytes=64)
         plane2 = keep.tile([P, S], U8, name="plane2", align_bytes=64)
@@ -56,17 +56,15 @@ def tile_list_tabhs_o_gelu_kernel(
         nc.vector.memset(win32[64:112, :], 0)
         nc.gpsimd.memset(w4_plane[:].rearrange("p a n -> p (a n)").bitcast(I32), 0)
         nc.gpsimd.memset(plane01[:].bitcast(I32), 0)
-        nc.gpsimd.memset(plane2[:].bitcast(I32), 0)
 
         nc.sync.dma_start(pick[:], offs)
         for a in (2, 0, 1):
             src = tab[a, 512 * T : 528 * T].rearrange("(q t) -> q t", q=16).bitcast(I32)
             nc.sync.dma_start(out=win32[rows_of_pass[a], :], in_=src)
         load_words(0)
-        nc.sync.dma_start(out=w8_raw[:], in_=w8.rearrange("(p j) n -> p j n", j=PACK))
         load_words(1)
+        nc.sync.dma_start(out=w8_raw[:], in_=w8.rearrange("(p j) n -> p j n", j=PACK))
         nc.sync.dma_start(place[:], offs2)
-        load_words(2)
 
         w4_plane32 = w4_plane[:].bitcast(I32)
         for q in range(QUADS):
@@ -77,20 +75,28 @@ def tile_list_tabhs_o_gelu_kernel(
         )
         nc.gpsimd.dma_start(out=bias[:], in_=b.rearrange("(p o) -> p o", o=1))
         nc.gpsimd.memset(page[:], 0.0)
+        nc.gpsimd.memset(plane2[:].bitcast(I32), 0)
 
         got_scales = keep.tile([P, S], U8, name="got_scales", align_bytes=64)
         nc.vector.tensor_copy(got_scales[:], scale_win[:].indirect(pick[:]))
         got32 = got_scales[:].bitcast(I32)
         planes = [(plane01, 4), (plane01, 0), (plane2, 0)]
-        for a in range(PASSES):
+
+        def move_plane(a, queues):
             plane, first = planes[a]
             rows = rows_of_pass[a]
-            for q in range(QUADS):
+            for q, queue in enumerate(queues):
                 lo = rows.start + 4 * q * rows.step
-                nc.sync.dma_start(
+                queue.dma_start(
                     out=plane[:].bitcast(I32)[32 * q + first : 32 * q + first + 4, :],
                     in_=got32[lo : lo + 3 * rows.step + 1 : rows.step, :],
                 )
+
+        move_plane(0, [nc.sync, nc.scalar, nc.scalar, nc.scalar])
+        words.append(keep.tile([P, T], U32, name="words2", tag="scales_then_words", align_bytes=64))
+        load_words(2)
+        move_plane(1, [nc.scalar] * QUADS)
+        move_plane(2, [nc.sync] * QUADS)
 
         nc.scalar.copy(out=w8_bf[:], in_=w8_raw[:].rearrange("p j n -> p n j"))
 

@@ -32,55 +32,34 @@ def tile_list_tabhs_o_gelu_kernel(
 
         pick = keep.tile([P, S // 16], U16, name="pick")
         place = keep.tile([P, S // 16], U16, name="place")
-        scale_win = keep.tile([P, T], U8, name="scale_win", tag="scales_then_words", align_bytes=64)
-        words = [keep.tile([P, T], U32, name="words%d" % a, align_bytes=64) for a in range(2)]
+        scale_win = keep.tile([P, T], U8, name="scale_win", tag="scales_then_words0", align_bytes=64)
+        words = {a: keep.tile([P, T], U32, name="words%d" % a, align_bytes=64) for a in (1, 2)}
         page = keep.tile([P, T], F32, name="page", align_bytes=64)
-        plane01 = keep.tile([P, S], U8, name="plane01", align_bytes=64)
+        plane10 = keep.tile([P, S], U8, name="plane10", align_bytes=64)
         plane2 = keep.tile([P, S], U8, name="plane2", align_bytes=64)
         w4_codes = keep.tile([P, 2, 2 * M], U8, name="w4_codes", align_bytes=64)
         w4_plane = keep.tile([P, 2, M], U8, name="w4_plane", align_bytes=64)
         bias = keep.tile([P, 1], F32, name="bias")
-        w8_raw = keep.tile([P, PACK, M], F32, name="w8_raw", tag="w8_then_wgo0", align_bytes=64)
-        w8_bf = keep.tile([P, M, PACK], BF16, name="w8_bf", tag="w8_then_wgo1", align_bytes=64)
+        w8_raw = keep.tile([P, PACK, M], F32, name="w8_raw", tag="then_gain0", align_bytes=64)
+        w8_bf = keep.tile([P, M, PACK], BF16, name="w8_bf", tag="w8_then_got", align_bytes=64)
         w8_codes = keep.tile([P, M], U32, name="w8_codes", align_bytes=64)
         w8_plane = keep.tile([P, M], U8, name="w8_plane", align_bytes=64)
+        got_scales = keep.tile([P, S], U8, name="got_scales", tag="then_gain1", align_bytes=64)
+        acc = [psum.tile([P, BANK], F32, name="acc%d" % s) for s in range(S // BANK)]
 
         win32 = scale_win[:].bitcast(I32)
-        rows_of_pass = [slice(0, 32, 2), slice(1, 32, 2), slice(112, 128, 1)]
+        got32 = got_scales[:].bitcast(I32)
+        w4_plane32 = w4_plane[:].bitcast(I32)
+        rows_of_pass = {1: slice(0, 32, 2), 2: slice(1, 32, 2), 0: slice(112, 128, 1)}
+        planes = {1: (plane10, 0), 2: (plane2, 0), 0: (plane10, 4)}
 
         def load_words(a):
             src = tab[a, 0 : 512 * T].rearrange("(p n) -> p n", p=P).bitcast(I32)
             nc.sync.dma_start(out=words[a][:].bitcast(I32), in_=src)
 
-        nc.vector.memset(win32[32:64, :], 0)
-        nc.vector.memset(win32[64:112, :], 0)
-        nc.gpsimd.memset(w4_plane[:].rearrange("p a n -> p (a n)").bitcast(I32), 0)
-        nc.gpsimd.memset(plane01[:].bitcast(I32), 0)
-
-        nc.sync.dma_start(pick[:], offs)
-        for a in (2, 0, 1):
-            src = tab[a, 512 * T : 528 * T].rearrange("(q t) -> q t", q=16).bitcast(I32)
-            nc.sync.dma_start(out=win32[rows_of_pass[a], :], in_=src)
-        load_words(0)
-        load_words(1)
-        nc.sync.dma_start(out=w8_raw[:], in_=w8.rearrange("(p j) n -> p j n", j=PACK))
-        nc.sync.dma_start(place[:], offs2)
-
-        w4_plane32 = w4_plane[:].bitcast(I32)
-        for q in range(QUADS):
+        def load_w4_scales(q):
             src = w4_scales[:, 4 * q : 4 * q + 4, :].rearrange("a r n -> r a n").bitcast(I32)
-            nc.gpsimd.dma_start(out=w4_plane32[32 * q : 32 * q + 4, :, :], in_=src)
-        nc.gpsimd.dma_start(
-            out=w4_codes[:].bitcast(I32), in_=w4_words.rearrange("a p n -> p a n").bitcast(I32)
-        )
-        nc.gpsimd.dma_start(out=bias[:], in_=b.rearrange("(p o) -> p o", o=1))
-        nc.gpsimd.memset(page[:], 0.0)
-        nc.gpsimd.memset(plane2[:].bitcast(I32), 0)
-
-        got_scales = keep.tile([P, S], U8, name="got_scales", align_bytes=64)
-        nc.vector.tensor_copy(got_scales[:], scale_win[:].indirect(pick[:]))
-        got32 = got_scales[:].bitcast(I32)
-        planes = [(plane01, 4), (plane01, 0), (plane2, 0)]
+            nc.sync.dma_start(out=w4_plane32[32 * q : 32 * q + 4, :, :], in_=src)
 
         def move_plane(a, queues):
             plane, first = planes[a]
@@ -92,71 +71,94 @@ def tile_list_tabhs_o_gelu_kernel(
                     in_=got32[lo : lo + 3 * rows.step + 1 : rows.step, :],
                 )
 
-        move_plane(0, [nc.sync, nc.scalar, nc.scalar, nc.scalar])
-        words.append(keep.tile([P, T], U32, name="words2", tag="scales_then_words", align_bytes=64))
+        def w4_pass(a, gathered):
+            for s in range(S // BANK):
+                cols = slice(s * BANK, (s + 1) * BANK)
+                nc.tensor.matmul_mx(
+                    out=acc[s][:],
+                    lhsT=w4_codes[:, a - 1, :].bitcast(FP4X4),
+                    lhsT_scale=w4_plane[:, a - 1, :],
+                    rhs=gathered[:, cols].bitcast(FP8X4),
+                    rhs_scale=planes[a][0][:, cols],
+                    start=(a == 1),
+                    stop=False,
+                )
+
+        nc.vector.memset(w4_plane[:].rearrange("p a n -> p (a n)").bitcast(I32), 0)
+        nc.vector.memset(win32[32:64, :], 0)
+        nc.vector.memset(win32[64:112, :], 0)
+        nc.vector.memset(plane10[:].bitcast(I32), 0)
+        nc.vector.memset(plane2[:].bitcast(I32), 0)
+        nc.vector.memset(page[:].bitcast(I32), 0)
+
+        nc.sync.dma_start(pick[:], offs)
+        for a in (0, 1, 2):
+            src = tab[a, 512 * T : 528 * T].rearrange("(q t) -> q t", q=16).bitcast(I32)
+            nc.sync.dma_start(out=win32[rows_of_pass[a], :], in_=src)
+        load_words(1)
+        nc.sync.dma_start(place[:], offs2)
+        nc.sync.dma_start(
+            out=w4_codes[:].bitcast(I32), in_=w4_words.rearrange("a p n -> p a n").bitcast(I32)
+        )
+        nc.sync.dma_start(out=bias[:], in_=b.rearrange("(p o) -> p o", o=1))
+        for q in range(QUADS - 1):
+            load_w4_scales(q)
         load_words(2)
-        move_plane(1, [nc.scalar] * QUADS)
-        move_plane(2, [nc.sync] * QUADS)
+        load_w4_scales(QUADS - 1)
+        nc.sync.dma_start(out=w8_raw[:], in_=w8.rearrange("(p j) n -> p j n", j=PACK))
+
+        nc.vector.tensor_copy(got_scales[:], scale_win[:].indirect(pick[:]))
+        move_plane(1, [nc.sync, nc.scalar, nc.scalar, nc.scalar])
+        words[0] = keep.tile([P, T], U32, name="words0", tag="scales_then_words0", align_bytes=64)
+        load_words(0)
+        move_plane(2, [nc.scalar] * QUADS)
 
         nc.scalar.copy(out=w8_bf[:], in_=w8_raw[:].rearrange("p j n -> p n j"))
 
-        got = [keep.tile([P, S], U32, name="got%d" % a, align_bytes=64) for a in range(2)]
-        got_last = [keep.tile([P, HALF], U32, name="got_last%d" % h, align_bytes=64) for h in range(2)]
-        nc.vector.tensor_copy(got[0][:], words[0][:].indirect(pick[:]))
+        for a in (1, 2):
+            gathered = keep.tile([P, S], U32, name="got%d" % a, align_bytes=64)
+            nc.vector.tensor_copy(gathered[:], words[a][:].indirect(pick[:]))
+            w4_pass(a, gathered)
+        move_plane(0, [nc.sync] * QUADS)
         nc.vector.quantize_mx(
             out=w8_codes[:].bitcast(FP8X4),
             scales=w8_plane[:],
             in_=w8_bf[:].rearrange("p n j -> p (n j)"),
         )
-        nc.vector.tensor_copy(got[1][:], words[1][:].indirect(pick[:]))
+
+        halves = [slice(h * HALF // 16, (h + 1) * HALF // 16) for h in range(2)]
+        got0 = [
+            keep.tile([P, HALF], U32, name="got0_%d" % h, tag=tag, align_bytes=64)
+            for h, tag in enumerate(("w8_then_got", "got0_1"))
+        ]
         for h in range(2):
-            cols16 = slice(h * HALF // 16, (h + 1) * HALF // 16)
-            nc.vector.tensor_copy(got_last[h][:], words[2][:].indirect(pick[:, cols16]))
+            nc.vector.tensor_copy(got0[h][:], words[0][:].indirect(pick[:, halves[h]]))
 
         for h in range(2):
-            gain = keep.tile([P, HALF], F32, name="gain%d" % h, tag="w8_then_wgo%d" % h, align_bytes=64)
+            gain = keep.tile([P, HALF], F32, name="gain%d" % h, tag="then_gain%d" % h, align_bytes=64)
             nc.sync.dma_start(out=gain[:], in_=wgo[:, h * HALF : (h + 1) * HALF])
             act = keep.tile([P, HALF], F32, name="act%d" % h, align_bytes=64)
             for s in range(HALF // BANK):
                 local = slice(s * BANK, (s + 1) * BANK)
                 cols = slice(h * HALF + s * BANK, h * HALF + (s + 1) * BANK)
-                acc = psum.tile([P, BANK], F32, name="acc%d_%d" % (h, s))
+                bank = acc[cols.start // BANK]
                 nc.tensor.matmul_mx(
-                    out=acc[:],
+                    out=bank[:],
                     lhsT=w8_codes[:].bitcast(FP8X4),
                     lhsT_scale=w8_plane[:],
-                    rhs=got[0][:, cols].bitcast(FP8X4),
-                    rhs_scale=plane01[4:P, cols],
-                    start=True,
-                    stop=False,
-                )
-                nc.tensor.matmul_mx(
-                    out=acc[:],
-                    lhsT=w4_codes[:, 0, :].bitcast(FP4X4),
-                    lhsT_scale=w4_plane[:, 0, :],
-                    rhs=got[1][:, cols].bitcast(FP8X4),
-                    rhs_scale=plane01[:, cols],
-                    start=False,
-                    stop=False,
-                )
-                nc.tensor.matmul_mx(
-                    out=acc[:],
-                    lhsT=w4_codes[:, 1, :].bitcast(FP4X4),
-                    lhsT_scale=w4_plane[:, 1, :],
-                    rhs=got_last[h][:, local].bitcast(FP8X4),
-                    rhs_scale=plane2[:, cols],
+                    rhs=got0[h][:, local].bitcast(FP8X4),
+                    rhs_scale=plane10[4:P, cols],
                     start=False,
                     stop=True,
                 )
                 nc.scalar.activation(
                     out=act[:, local],
-                    in_=acc[:],
+                    in_=bank[:],
                     func=mybir.ActivationFunctionType.Gelu_apprx_tanh,
                     bias=bias[:],
                 )
-            cols16 = slice(h * HALF // 16, (h + 1) * HALF // 16)
             nc.vector.tensor_tensor(
-                page[:].indirect(place[:, cols16]), act[:], gain[:], mybir.AluOpType.mult
+                page[:].indirect(place[:, halves[h]]), act[:], gain[:], mybir.AluOpType.mult
             )
 
         nc.sync.dma_start(out=out, in_=page[:])

@@ -32,11 +32,10 @@ def tile_list_tabhs_o_gelu_kernel(
 
         pick = keep.tile([P, S // 16], U16, name="pick")
         place = keep.tile([P, S // 16], U16, name="place")
-        scale_win = keep.tile([P, T], U8, name="scale_win", tag="scales_then_words0", align_bytes=64)
-        words = {a: keep.tile([P, T], U32, name="words%d" % a, align_bytes=64) for a in (1, 2)}
-        page = keep.tile([P, T], F32, name="page", align_bytes=64)
-        plane10 = keep.tile([P, S], U8, name="plane10", align_bytes=64)
-        plane2 = keep.tile([P, S], U8, name="plane2", align_bytes=64)
+        scale_win = keep.tile([P, T], U8, name="scale_win", tag="scales_then_page", align_bytes=64)
+        words = [keep.tile([P, T], U32, name="words%d" % a, align_bytes=64) for a in range(PASSES)]
+        planes = [keep.tile([P, S], U8, name="plane%d" % a, align_bytes=64) for a in range(PASSES)]
+        warm = keep.tile([P, 2], F32, name="warm")
         w4_codes = keep.tile([P, 2, 2 * M], U8, name="w4_codes", align_bytes=64)
         w4_plane = keep.tile([P, 2, M], U8, name="w4_plane", align_bytes=64)
         bias = keep.tile([P, 1], F32, name="bias")
@@ -51,23 +50,17 @@ def tile_list_tabhs_o_gelu_kernel(
         got32 = got_scales[:].bitcast(I32)
         w4_plane32 = w4_plane[:].bitcast(I32)
         rows_of_pass = {1: slice(0, 32, 2), 2: slice(1, 32, 2), 0: slice(112, 128, 1)}
-        planes = {1: (plane10, 0), 2: (plane2, 0), 0: (plane10, 4)}
 
         def load_words(a):
             src = tab[a, 0 : 512 * T].rearrange("(p n) -> p n", p=P).bitcast(I32)
             nc.sync.dma_start(out=words[a][:].bitcast(I32), in_=src)
 
-        def load_w4_scales(q):
-            src = w4_scales[:, 4 * q : 4 * q + 4, :].rearrange("a r n -> r a n").bitcast(I32)
-            nc.sync.dma_start(out=w4_plane32[32 * q : 32 * q + 4, :, :], in_=src)
-
-        def move_plane(a, queues):
-            plane, first = planes[a]
+        def move_plane(a, queue):
             rows = rows_of_pass[a]
-            for q, queue in enumerate(queues):
+            for q in range(QUADS):
                 lo = rows.start + 4 * q * rows.step
                 queue.dma_start(
-                    out=plane[:].bitcast(I32)[32 * q + first : 32 * q + first + 4, :],
+                    out=planes[a][:].bitcast(I32)[32 * q : 32 * q + 4, :],
                     in_=got32[lo : lo + 3 * rows.step + 1 : rows.step, :],
                 )
 
@@ -79,39 +72,43 @@ def tile_list_tabhs_o_gelu_kernel(
                     lhsT=w4_codes[:, a - 1, :].bitcast(FP4X4),
                     lhsT_scale=w4_plane[:, a - 1, :],
                     rhs=gathered[:, cols].bitcast(FP8X4),
-                    rhs_scale=planes[a][0][:, cols],
+                    rhs_scale=planes[a][:, cols],
                     start=(a == 1),
                     stop=False,
                 )
 
-        nc.vector.memset(w4_plane[:].rearrange("p a n -> p (a n)").bitcast(I32), 0)
+        nc.vector.memset(warm[:, 0:1], 0.0)
+        nc.scalar.activation(out=warm[:, 1:2], in_=warm[:, 0:1], func=mybir.ActivationFunctionType.Gelu_apprx_tanh)
         nc.vector.memset(win32[32:64, :], 0)
-        nc.vector.memset(win32[64:112, :], 0)
-        nc.vector.memset(plane10[:].bitcast(I32), 0)
-        nc.vector.memset(plane2[:].bitcast(I32), 0)
-        nc.vector.memset(page[:].bitcast(I32), 0)
+        nc.vector.memset(planes[1][:].bitcast(I32), 0)
+        nc.vector.memset(planes[0][:].bitcast(I32), 0)
+        nc.gpsimd.memset(win32[64:112, :], 0)
+        nc.gpsimd.memset(w4_plane[:].rearrange("p a n -> p (a n)").bitcast(I32), 0)
+        nc.gpsimd.memset(planes[2][:].bitcast(I32), 0)
 
         nc.sync.dma_start(pick[:], offs)
         for a in (0, 1, 2):
             src = tab[a, 512 * T : 528 * T].rearrange("(q t) -> q t", q=16).bitcast(I32)
             nc.sync.dma_start(out=win32[rows_of_pass[a], :], in_=src)
-        load_words(1)
+        for a in (1, 2, 0):
+            load_words(a)
+        nc.sync.dma_start(out=w8_raw[:], in_=w8.rearrange("(p j) n -> p j n", j=PACK))
         nc.sync.dma_start(place[:], offs2)
-        nc.sync.dma_start(
+
+        for q in range(QUADS):
+            src = w4_scales[:, 4 * q : 4 * q + 4, :].rearrange("a r n -> r a n").bitcast(I32)
+            nc.gpsimd.dma_start(out=w4_plane32[32 * q : 32 * q + 4, :, :], in_=src)
+        nc.gpsimd.dma_start(
             out=w4_codes[:].bitcast(I32), in_=w4_words.rearrange("a p n -> p a n").bitcast(I32)
         )
-        nc.sync.dma_start(out=bias[:], in_=b.rearrange("(p o) -> p o", o=1))
-        for q in range(QUADS - 1):
-            load_w4_scales(q)
-        load_words(2)
-        load_w4_scales(QUADS - 1)
-        nc.sync.dma_start(out=w8_raw[:], in_=w8.rearrange("(p j) n -> p j n", j=PACK))
+        nc.gpsimd.dma_start(out=bias[:], in_=b.rearrange("(p o) -> p o", o=1))
 
         nc.vector.tensor_copy(got_scales[:], scale_win[:].indirect(pick[:]))
-        move_plane(1, [nc.sync, nc.scalar, nc.scalar, nc.scalar])
-        words[0] = keep.tile([P, T], U32, name="words0", tag="scales_then_words0", align_bytes=64)
-        load_words(0)
-        move_plane(2, [nc.scalar] * QUADS)
+        move_plane(1, nc.scalar)
+        move_plane(0, nc.scalar)
+        move_plane(2, nc.gpsimd)
+        page = keep.tile([P, T], F32, name="page", tag="scales_then_page", align_bytes=64)
+        nc.gpsimd.memset(page[:], 0.0)
 
         nc.scalar.copy(out=w8_bf[:], in_=w8_raw[:].rearrange("p j n -> p n j"))
 
@@ -119,7 +116,6 @@ def tile_list_tabhs_o_gelu_kernel(
             gathered = keep.tile([P, S], U32, name="got%d" % a, align_bytes=64)
             nc.vector.tensor_copy(gathered[:], words[a][:].indirect(pick[:]))
             w4_pass(a, gathered)
-        move_plane(0, [nc.sync] * QUADS)
         nc.vector.quantize_mx(
             out=w8_codes[:].bitcast(FP8X4),
             scales=w8_plane[:],
@@ -129,7 +125,7 @@ def tile_list_tabhs_o_gelu_kernel(
         halves = [slice(h * HALF // 16, (h + 1) * HALF // 16) for h in range(2)]
         got0 = [
             keep.tile([P, HALF], U32, name="got0_%d" % h, tag=tag, align_bytes=64)
-            for h, tag in enumerate(("w8_then_got", "got0_1"))
+            for h, tag in enumerate(("got0_0", "w8_then_got"))
         ]
         for h in range(2):
             nc.vector.tensor_copy(got0[h][:], words[0][:].indirect(pick[:, halves[h]]))
@@ -147,7 +143,7 @@ def tile_list_tabhs_o_gelu_kernel(
                     lhsT=w8_codes[:].bitcast(FP8X4),
                     lhsT_scale=w8_plane[:],
                     rhs=got0[h][:, local].bitcast(FP8X4),
-                    rhs_scale=plane10[4:P, cols],
+                    rhs_scale=planes[0][:, cols],
                     start=False,
                     stop=True,
                 )

from contextlib import ExitStack

import concourse.mybir as mybir

K, M, T, S = 1536, 128, 4096, 2048
FLOPS = 2 * K * M * S

F32 = mybir.dt.float32
BF16 = mybir.dt.bfloat16
I32 = mybir.dt.int32
U32 = mybir.dt.uint32
U16 = mybir.dt.uint16
U8 = mybir.dt.uint8
FP8X4 = mybir.dt.float8_e4m3fn_x4
FP4X4 = mybir.dt.float4_e2m1fn_x4

P = 128
PACK = 4
PASSES = 3
BANK = 512
HALF = S // 2
QUADS = 4


def tile_list_tabhs_o_gelu_kernel(
    tc, tab, w8, w4_words, w4_scales, b, wgo, offs, offs2, out
):
    nc = tc.nc
    with ExitStack() as ctx:
        keep = ctx.enter_context(tc.tile_pool(name="keep", bufs=1))
        psum = ctx.enter_context(tc.psum_pool(name="psum", bufs=1))

        pick = keep.tile([P, S // 16], U16, name="pick")
        place = keep.tile([P, S // 16], U16, name="place")
        scale_win = keep.tile([P, T], U8, name="scale_win", tag="scales_then_page", align_bytes=64)
        words = [keep.tile([P, T], U32, name="words%d" % a, align_bytes=64) for a in range(PASSES)]
        planes = [keep.tile([P, S], U8, name="plane%d" % a, align_bytes=64) for a in range(PASSES)]
        warm = keep.tile([P, 2], F32, name="warm")
        w4_codes = keep.tile([P, 2, 2 * M], U8, name="w4_codes", align_bytes=64)
        w4_plane = keep.tile([P, 2, M], U8, name="w4_plane", align_bytes=64)
        bias = keep.tile([P, 1], F32, name="bias")
        w8_raw = keep.tile([P, PACK, M], F32, name="w8_raw", tag="then_gain0", align_bytes=64)
        w8_bf = keep.tile([P, M, PACK], BF16, name="w8_bf", tag="w8_then_got", align_bytes=64)
        w8_codes = keep.tile([P, M], U32, name="w8_codes", align_bytes=64)
        w8_plane = keep.tile([P, M], U8, name="w8_plane", align_bytes=64)
        got_scales = keep.tile([P, S], U8, name="got_scales", tag="then_gain1", align_bytes=64)
        acc = [psum.tile([P, BANK], F32, name="acc%d" % s) for s in range(S // BANK)]

        win32 = scale_win[:].bitcast(I32)
        got32 = got_scales[:].bitcast(I32)
        w4_plane32 = w4_plane[:].bitcast(I32)
        rows_of_pass = {1: slice(0, 32, 2), 2: slice(1, 32, 2), 0: slice(112, 128, 1)}

        def load_words(a):
            src = tab[a, 0 : 512 * T].rearrange("(p n) -> p n", p=P).bitcast(I32)
            nc.sync.dma_start(out=words[a][:].bitcast(I32), in_=src)

        def move_plane(a, queue):
            rows = rows_of_pass[a]
            for q in range(QUADS):
                lo = rows.start + 4 * q * rows.step
                queue.dma_start(
                    out=planes[a][:].bitcast(I32)[32 * q : 32 * q + 4, :],
                    in_=got32[lo : lo + 3 * rows.step + 1 : rows.step, :],
                )

        def w4_pass(a, gathered):
            for s in range(S // BANK):
                cols = slice(s * BANK, (s + 1) * BANK)
                nc.tensor.matmul_mx(
                    out=acc[s][:],
                    lhsT=w4_codes[:, a - 1, :].bitcast(FP4X4),
                    lhsT_scale=w4_plane[:, a - 1, :],
                    rhs=gathered[:, cols].bitcast(FP8X4),
                    rhs_scale=planes[a][:, cols],
                    start=(a == 1),
                    stop=False,
                )

        nc.vector.memset(warm[:, 0:1], 0.0)
        nc.scalar.activation(out=warm[:, 1:2], in_=warm[:, 0:1], func=mybir.ActivationFunctionType.Gelu_apprx_tanh)
        nc.vector.memset(win32[32:64, :], 0)
        nc.vector.memset(planes[1][:].bitcast(I32), 0)
        nc.vector.memset(planes[0][:].bitcast(I32), 0)
        nc.gpsimd.memset(win32[64:112, :], 0)
        nc.gpsimd.memset(w4_plane[:].rearrange("p a n -> p (a n)").bitcast(I32), 0)
        nc.gpsimd.memset(planes[2][:].bitcast(I32), 0)

        nc.sync.dma_start(pick[:], offs)
        for a in (0, 1, 2):
            src = tab[a, 512 * T : 528 * T].rearrange("(q t) -> q t", q=16).bitcast(I32)
            nc.sync.dma_start(out=win32[rows_of_pass[a], :], in_=src)
        for a in (1, 2, 0):
            load_words(a)
        nc.sync.dma_start(out=w8_raw[:], in_=w8.rearrange("(p j) n -> p j n", j=PACK))
        nc.sync.dma_start(place[:], offs2)

        for q in range(QUADS):
            src = w4_scales[:, 4 * q : 4 * q + 4, :].rearrange("a r n -> r a n").bitcast(I32)
            nc.gpsimd.dma_start(out=w4_plane32[32 * q : 32 * q + 4, :, :], in_=src)
        nc.gpsimd.dma_start(
            out=w4_codes[:].bitcast(I32), in_=w4_words.rearrange("a p n -> p a n").bitcast(I32)
        )
        nc.gpsimd.dma_start(out=bias[:], in_=b.rearrange("(p o) -> p o", o=1))

        nc.vector.tensor_copy(got_scales[:], scale_win[:].indirect(pick[:]))
        move_plane(1, nc.scalar)
        move_plane(0, nc.scalar)
        move_plane(2, nc.gpsimd)
        page = keep.tile([P, T], F32, name="page", tag="scales_then_page", align_bytes=64)
        nc.gpsimd.memset(page[:], 0.0)

        nc.scalar.copy(out=w8_bf[:], in_=w8_raw[:].rearrange("p j n -> p n j"))

        for a in (1, 2):
            gathered = keep.tile([P, S], U32, name="got%d" % a, align_bytes=64)
            nc.vector.tensor_copy(gathered[:], words[a][:].indirect(pick[:]))
            w4_pass(a, gathered)
        nc.vector.quantize_mx(
            out=w8_codes[:].bitcast(FP8X4),
            scales=w8_plane[:],
            in_=w8_bf[:].rearrange("p n j -> p (n j)"),
        )

        halves = [slice(h * HALF // 16, (h + 1) * HALF // 16) for h in range(2)]
        got0 = [
            keep.tile([P, HALF], U32, name="got0_%d" % h, tag=tag, align_bytes=64)
            for h, tag in enumerate(("got0_0", "w8_then_got"))
        ]
        for h in range(2):
            nc.vector.tensor_copy(got0[h][:], words[0][:].indirect(pick[:, halves[h]]))

        for h in range(2):
            gain = keep.tile([P, HALF], F32, name="gain%d" % h, tag="then_gain%d" % h, align_bytes=64)
            nc.sync.dma_start(out=gain[:], in_=wgo[:, h * HALF : (h + 1) * HALF])
            act = keep.tile([P, HALF], F32, name="act%d" % h, align_bytes=64)
            for s in range(HALF // BANK):
                local = slice(s * BANK, (s + 1) * BANK)
                cols = slice(h * HALF + s * BANK, h * HALF + (s + 1) * BANK)
                bank = acc[cols.start // BANK]
                nc.tensor.matmul_mx(
                    out=bank[:],
                    lhsT=w8_codes[:].bitcast(FP8X4),
                    lhsT_scale=w8_plane[:],
                    rhs=got0[h][:, local].bitcast(FP8X4),
                    rhs_scale=planes[0][:, cols],
                    start=False,
                    stop=True,
                )
                nc.scalar.activation(
                    out=act[:, local],
                    in_=bank[:],
                    func=mybir.ActivationFunctionType.Gelu_apprx_tanh,
                    bias=bias[:],
                )
            nc.vector.tensor_tensor(
                page[:].indirect(place[:, halves[h]]), act[:], gain[:], mybir.AluOpType.mult
            )

        nc.sync.dma_start(out=out, in_=page[:])
